import numpy as np
import ml_dtypes


def mxq(x, axis, fmt="e4m3"):
    dtype, down = {"e4m3": (ml_dtypes.float8_e4m3fn, 7), "e5m2": (ml_dtypes.float8_e5m2, 14)}[fmt]
    v = np.moveaxis(np.asarray(x, np.float32).astype(ml_dtypes.bfloat16).astype(np.float64), axis, -1)
    blocks = v.reshape(v.shape[:-1] + (-1, 32))
    amax = np.abs(blocks).max(-1, keepdims=True)
    byte = np.maximum(np.where(amax > 0, np.frexp(amax)[1] - 1 + 127, 0) - down, 1)
    scale = np.exp2(byte - 127.0)
    codes = (blocks / scale).astype(np.float32).astype(dtype).astype(np.float64)
    return np.moveaxis((codes * scale).reshape(v.shape), -1, axis)


WIDE = False


def mx_kscale(k):
    if not WIDE:
        return np.ones(k)
    levels = np.array([10, -10, 5, -5, 0])
    if k % 512:
        return np.exp2(np.random.permutation(np.resize(levels, k // 32))).repeat(32)
    a = np.empty((k // 512, 16))
    for p in range(k // 512):
        a[p, :8] = np.random.permutation(np.resize(levels, 8))
        for g in range(8):
            far = levels[np.abs(levels - a[p, g]) >= 10]
            a[p, g + 8] = far[np.random.randint(len(far))]
    return np.exp2(a.ravel()).repeat(32)


def f64(x):
    return np.asarray(x).astype(np.float64)


def striped(idx):
    return np.tile(idx.reshape(-1, 16).T, (8, 1)).astype(np.uint16)


def unstriped(offs):
    return offs[:16].T.reshape(-1).astype(np.int64)


K, T, E, C, N = 512, 4096, 8, 128, 128


def by_expert(wq, xq):
    return np.concatenate([wq[e].T @ xq[:, e * C:(e + 1) * C] for e in range(E)], axis=1)


def setup_inputs():
    n = np.random.standard_normal
    s = mx_kscale(K)[:, None]
    return {
        "xT": (n((K, T)) * s).astype(np.float32),
        "w": (n((E, K, N)) / np.sqrt(K) / s[None]).astype(np.float32),
        "gate": np.tile(np.random.uniform(0.2, 1.0, E * C), (N, 1)).astype(np.float32),
        "offs": striped(np.random.permutation(T)[:E * C]),
    }


def reference(xT, w, gate, offs):
    idx = unstriped(offs)
    xq = mxq(f64(xT)[:, idx], 0, "e4m3")
    y = by_expert(mxq(f64(w), 1, "e4m3"), xq)
    out = np.zeros((N, T))
    out[:, idx] = f64(gate) * y
    return out

@@ -1,0 +1,145 @@
+from contextlib import ExitStack
+
+import concourse.mybir as mybir
+
+K, T, E, C, N = 512, 4096, 8, 128, 128
+SLOTS = E * C
+
+FLOPS = 2 * K * N * SLOTS
+
+F32 = mybir.dt.float32
+BF16 = mybir.dt.bfloat16
+U32 = mybir.dt.uint32
+U16 = mybir.dt.uint16
+U8 = mybir.dt.uint8
+FP8X4 = mybir.dt.float8_e4m3fn_x4
+
+P = 128
+PACK = 4
+HALVES = 2
+H_SLOTS = SLOTS // HALVES
+H_EXPERTS = E // HALVES
+H_COLS = H_SLOTS // 16
+
+
+def tile_routed_moe_kernel(tc, xT, w, gate, offs, out):
+    nc = tc.nc
+    mult = mybir.AluOpType.mult
+    add = mybir.AluOpType.add
+
+    with ExitStack() as ctx:
+        held = ctx.enter_context(tc.tile_pool(name="held", bufs=1))
+        psum = ctx.enter_context(tc.psum_pool(name="psum", bufs=1))
+
+        offsets = held.tile([P, SLOTS // 16], U16, name="offsets")
+        nc.sync.dma_start(offsets[:], offs)
+
+        x_view = xT.rearrange("(p t) n -> p t n", t=PACK)
+        planes = []
+        for t in range(PACK):
+            plane = held.tile([P, T], F32, name="plane%d" % t)
+            nc.sync.dma_start(plane[:], x_view[:, t, :])
+            planes.append(plane)
+
+        w_view = w.rearrange("e (p j) n -> p e (j n)", j=PACK)
+        w_raw = []
+        for q in range(E // 2):
+            raw = held.tile([P, 2, PACK, N], F32, name="w_raw%d" % q)
+            nc.sync.dma_start(raw[:].rearrange("p e j n -> p e (j n)"), w_view[:, 2 * q : 2 * q + 2, :])
+            w_raw.append(raw)
+
+        gate_sb = held.tile([P, SLOTS], F32, name="gate_sb")
+        nc.sync.dma_start(gate_sb[:], gate)
+
+        warm_in = held.tile([P, 8], F32, name="warm_in")
+        warm_out = held.tile([P, 8], F32, name="warm_out")
+        nc.gpsimd.memset(warm_in[:], 0.0)
+        nc.scalar.copy(warm_out[:], warm_in[:])
+
+        window = held.tile([P, T], F32, name="window")
+        nc.vector.memset(window[:], 0.0)
+
+        x_grouped = [
+            held.tile([P, H_SLOTS, PACK], BF16, name="x_grouped%d" % h, align_bytes=64) for h in range(HALVES)
+        ]
+        for t in range(PACK):
+            for h in range(HALVES):
+                nc.vector.tensor_copy(
+                    x_grouped[h][:, :, t],
+                    planes[t][:].indirect(offsets[:, h * H_COLS : (h + 1) * H_COLS]),
+                )
+
+        x_codes, x_scales = [], []
+        for h in range(HALVES):
+            codes = held.tile([P, H_SLOTS], U32, name="x_codes%d" % h, align_bytes=64)
+            scales = held.tile([P, H_SLOTS], U8, name="x_scales%d" % h, align_bytes=64)
+            nc.vector.quantize_mx(
+                out=codes[:].bitcast(FP8X4),
+                scales=scales[:],
+                in_=x_grouped[h][:].rearrange("p n j -> p (n j)"),
+            )
+            x_codes.append(codes)
+            x_scales.append(scales)
+
+        w_grouped = [
+            held.tile([P, H_EXPERTS, N, PACK], BF16, name="w_grouped%d" % h, align_bytes=64) for h in range(HALVES)
+        ]
+
+        def views(q):
+            dst = w_grouped[q // 2][:, 2 * (q % 2) : 2 * (q % 2) + 2, :, :]
+            src = w_raw[q][:]
+            return dst, src.rearrange("p e j n -> p e n j")
+
+        def interleave(engine_copy, q):
+            dst, src = views(q)
+            engine_copy(dst, src)
+
+        def interleave_gpsimd(q):
+            dst, src = views(q)
+            nc.gpsimd.tensor_scalar(dst, src, 1.0, 0.0, op0=mult, op1=add)
+
+        w_codes = [held.tile([P, H_EXPERTS * N], U32, name="w_codes%d" % h, align_bytes=64) for h in range(HALVES)]
+        w_scales = [held.tile([P, H_EXPERTS * N], U8, name="w_scales%d" % h, align_bytes=64) for h in range(HALVES)]
+
+        def quantize_w(h):
+            nc.vector.quantize_mx(
+                out=w_codes[h][:].bitcast(FP8X4),
+                scales=w_scales[h][:],
+                in_=w_grouped[h][:].rearrange("p e n j -> p (e n j)"),
+            )
+
+        sums = [held.tile([P, H_SLOTS], F32, name="sums%d" % h) for h in range(HALVES)]
+
+        def multiply(h):
+            acc = psum.tile([P, H_SLOTS], F32, name="acc%d" % h)
+            for c in range(H_EXPERTS):
+                cols = slice(c * C, (c + 1) * C)
+                nc.tensor.matmul_mx(
+                    out=acc[:, cols],
+                    lhsT=w_codes[h][:, cols].bitcast(FP8X4),
+                    lhsT_scale=w_scales[h][:, cols],
+                    rhs=x_codes[h][:, cols].bitcast(FP8X4),
+                    rhs_scale=x_scales[h][:, cols],
+                    start=True,
+                    stop=True,
+                )
+            nc.scalar.copy(sums[h][:], acc[:])
+
+        interleave(nc.scalar.copy, 0)
+        interleave(nc.scalar.copy, 1)
+        interleave(nc.scalar.copy, 2)
+        quantize_w(0)
+        multiply(0)
+        interleave(nc.vector.tensor_copy, 3)
+        quantize_w(1)
+        multiply(1)
+
+        for h in range(HALVES):
+            nc.vector.tensor_tensor(
+                window[:].indirect(offsets[:, h * H_COLS : (h + 1) * H_COLS]),
+                sums[h][:],
+                gate_sb[:, h * H_SLOTS : (h + 1) * H_SLOTS],
+                mult,
+            )
+
+        nc.sync.dma_start(out, window[:])

@@ -108,6 +108,14 @@ def tile_routed_moe_kernel(tc, xT, w, gate, offs, out):
                 in_=w_grouped[h][:].rearrange("p e n j -> p (e n j)"),
             )
 
+        def quantize_pair(q):
+            h, lo = q // 2, 2 * (q % 2)
+            nc.vector.quantize_mx(
+                out=w_codes[h][:, lo * N : (lo + 2) * N].bitcast(FP8X4),
+                scales=w_scales[h][:, lo * N : (lo + 2) * N],
+                in_=w_grouped[h][:, lo : lo + 2, :, :].rearrange("p e n j -> p (e n j)"),
+            )
+
         sums = [held.tile([P, H_SLOTS], F32, name="sums%d" % h) for h in range(HALVES)]
 
         def multiply(h):
@@ -131,7 +139,8 @@ def tile_routed_moe_kernel(tc, xT, w, gate, offs, out):
         quantize_w(0)
         multiply(0)
         interleave(nc.vector.tensor_copy, 3)
-        quantize_w(1)
+        quantize_pair(2)
+        quantize_pair(3)
         multiply(1)
 
         for h in range(HALVES):

@@ -49,7 +49,8 @@ def tile_routed_moe_kernel(tc, xT, w, gate, offs, out):
             w_raw.append(raw)
 
         gate_sb = held.tile([P, SLOTS], F32, name="gate_sb")
-        nc.sync.dma_start(gate_sb[:], gate)
+        for h in range(HALVES):
+            nc.sync.dma_start(gate_sb[:, h * H_SLOTS : (h + 1) * H_SLOTS], gate[:, h * H_SLOTS : (h + 1) * H_SLOTS])
 
         warm_in = held.tile([P, 8], F32, name="warm_in")
         warm_out = held.tile([P, 8], F32, name="warm_out")

@@ -32,14 +32,16 @@ def tile_routed_moe_kernel(tc, xT, w, gate, offs, out):
         psum = ctx.enter_context(tc.psum_pool(name="psum", bufs=1))
 
         offsets = held.tile([P, SLOTS // 16], U16, name="offsets")
-        nc.sync.dma_start(offsets[:], offs)
 
         x_view = xT.rearrange("(p t) n -> p t n", t=PACK)
         planes = []
         for t in range(PACK):
             plane = held.tile([P, T], F32, name="plane%d" % t)
-            nc.sync.dma_start(plane[:], x_view[:, t, :])
+            nc.sync.dma_start(plane[:, : T // 2], x_view[:, t, : T // 2])
+            nc.sync.dma_start(plane[:, T // 2 :], x_view[:, t, T // 2 :])
             planes.append(plane)
+            if t == 0:
+                nc.sync.dma_start(offsets[:], offs)
 
         w_view = w.rearrange("e (p j) n -> p e (j n)", j=PACK)
         w_raw = []

@@ -139,7 +139,8 @@ def tile_routed_moe_kernel(tc, xT, w, gate, offs, out):
         interleave(nc.scalar.copy, 0)
         interleave(nc.scalar.copy, 1)
         interleave(nc.scalar.copy, 2)
-        quantize_w(0)
+        quantize_pair(0)
+        quantize_pair(1)
         multiply(0)
         interleave(nc.vector.tensor_copy, 3)
         quantize_pair(2)

@@ -46,7 +46,7 @@ def tile_routed_moe_kernel(tc, xT, w, gate, offs, out):
         w_view = w.rearrange("e (p j) n -> p e (j n)", j=PACK)
         w_raw = []
         for q in range(E // 2):
-            raw = held.tile([P, 2, PACK, N], F32, name="w_raw%d" % q)
+            raw = held.tile([P, 2, PACK, N], F32, name="w_raw%d" % q, align_bytes=64)
             nc.sync.dma_start(raw[:].rearrange("p e j n -> p e (j n)"), w_view[:, 2 * q : 2 * q + 2, :])
             w_raw.append(raw)
 
@@ -71,18 +71,6 @@ def tile_routed_moe_kernel(tc, xT, w, gate, offs, out):
                     x_grouped[h][:, :, t],
                     planes[t][:].indirect(offsets[:, h * H_COLS : (h + 1) * H_COLS]),
                 )
-
-        x_codes, x_scales = [], []
-        for h in range(HALVES):
-            codes = held.tile([P, H_SLOTS], U32, name="x_codes%d" % h, align_bytes=64)
-            scales = held.tile([P, H_SLOTS], U8, name="x_scales%d" % h, align_bytes=64)
-            nc.vector.quantize_mx(
-                out=codes[:].bitcast(FP8X4),
-                scales=scales[:],
-                in_=x_grouped[h][:].rearrange("p n j -> p (n j)"),
-            )
-            x_codes.append(codes)
-            x_scales.append(scales)
 
         w_grouped = [
             held.tile([P, H_EXPERTS, N, PACK], BF16, name="w_grouped%d" % h, align_bytes=64) for h in range(HALVES)
@@ -119,6 +107,17 @@ def tile_routed_moe_kernel(tc, xT, w, gate, offs, out):
                 in_=w_grouped[h][:, lo : lo + 2, :, :].rearrange("p e n j -> p (e n j)"),
             )
 
+        x_codes, x_scales = [None, None], [None, None]
+
+        def quantize_x(h, tag):
+            x_codes[h] = held.tile([P, H_SLOTS], U32, name=tag, align_bytes=64)
+            x_scales[h] = held.tile([P, H_SLOTS], U8, name="x_scales%d" % h, align_bytes=64)
+            nc.vector.quantize_mx(
+                out=x_codes[h][:].bitcast(FP8X4),
+                scales=x_scales[h][:],
+                in_=x_grouped[h][:].rearrange("p n j -> p (n j)"),
+            )
+
         sums = [held.tile([P, H_SLOTS], F32, name="sums%d" % h) for h in range(HALVES)]
 
         def multiply(h):
@@ -139,8 +138,10 @@ def tile_routed_moe_kernel(tc, xT, w, gate, offs, out):
         interleave(nc.scalar.copy, 0)
         interleave(nc.scalar.copy, 1)
         interleave(nc.scalar.copy, 2)
+        quantize_x(0, "x_codes0")
         quantize_pair(0)
         quantize_pair(1)
+        quantize_x(1, "w_raw1")
         multiply(0)
         interleave(nc.vector.tensor_copy, 3)
         quantize_pair(2)

@@ -79,7 +79,10 @@ def tile_routed_moe_kernel(tc, xT, w, gate, offs, out):
         def views(q):
             dst = w_grouped[q // 2][:, 2 * (q % 2) : 2 * (q % 2) + 2, :, :]
             src = w_raw[q][:]
-            return dst, src.rearrange("p e j n -> p e n j")
+            return (
+                dst.rearrange("p e (c i) j -> p e c j i", i=4),
+                src.rearrange("p e j (c i) -> p e c j i", i=4),
+            )
 
         def interleave(engine_copy, q):
             dst, src = views(q)

@@ -25,7 +25,6 @@ H_COLS = H_SLOTS // 16
 def tile_routed_moe_kernel(tc, xT, w, gate, offs, out):
     nc = tc.nc
     mult = mybir.AluOpType.mult
-    add = mybir.AluOpType.add
 
     with ExitStack() as ctx:
         held = ctx.enter_context(tc.tile_pool(name="held", bufs=1))
@@ -43,11 +42,11 @@ def tile_routed_moe_kernel(tc, xT, w, gate, offs, out):
             if t == 0:
                 nc.sync.dma_start(offsets[:], offs)
 
-        w_view = w.rearrange("e (p j) n -> p e (j n)", j=PACK)
+        w_view = w.rearrange("e (p j) n -> e p (j n)", j=PACK)
         w_raw = []
-        for q in range(E // 2):
-            raw = held.tile([P, 2, PACK, N], F32, name="w_raw%d" % q, align_bytes=64)
-            nc.sync.dma_start(raw[:].rearrange("p e j n -> p e (j n)"), w_view[:, 2 * q : 2 * q + 2, :])
+        for e in range(E):
+            raw = held.tile([P, PACK, N], F32, name="w_raw%d" % e, align_bytes=64)
+            nc.sync.dma_start(raw[:].rearrange("p j n -> p (j n)"), w_view[e])
             w_raw.append(raw)
 
         gate_sb = held.tile([P, SLOTS], F32, name="gate_sb")
@@ -62,45 +61,24 @@ def tile_routed_moe_kernel(tc, xT, w, gate, offs, out):
         window = held.tile([P, T], F32, name="window")
         nc.vector.memset(window[:], 0.0)
 
-        x_grouped = [
-            held.tile([P, H_SLOTS, PACK], BF16, name="x_grouped%d" % h, align_bytes=64) for h in range(HALVES)
-        ]
+        x_grouped = held.tile([P, SLOTS, PACK], BF16, name="x_grouped", align_bytes=64)
         for t in range(PACK):
-            for h in range(HALVES):
-                nc.vector.tensor_copy(
-                    x_grouped[h][:, :, t],
-                    planes[t][:].indirect(offsets[:, h * H_COLS : (h + 1) * H_COLS]),
-                )
+            nc.vector.tensor_copy(x_grouped[:, :, t], planes[t][:].indirect(offsets[:]))
 
         w_grouped = [
             held.tile([P, H_EXPERTS, N, PACK], BF16, name="w_grouped%d" % h, align_bytes=64) for h in range(HALVES)
         ]
 
-        def views(q):
-            dst = w_grouped[q // 2][:, 2 * (q % 2) : 2 * (q % 2) + 2, :, :]
-            src = w_raw[q][:]
-            return (
-                dst.rearrange("p e (c i) j -> p e c j i", i=4),
-                src.rearrange("p e j (c i) -> p e c j i", i=4),
+        def interleave(engine_copy, e):
+            dst = w_grouped[e // H_EXPERTS][:, e % H_EXPERTS, :, :]
+            src = w_raw[e][:]
+            engine_copy(
+                dst.rearrange("p (g c i) j -> p g c j i", g=2, i=4),
+                src.rearrange("p j (g c i) -> p g c j i", g=2, i=4),
             )
-
-        def interleave(engine_copy, q):
-            dst, src = views(q)
-            engine_copy(dst, src)
-
-        def interleave_gpsimd(q):
-            dst, src = views(q)
-            nc.gpsimd.tensor_scalar(dst, src, 1.0, 0.0, op0=mult, op1=add)
 
         w_codes = [held.tile([P, H_EXPERTS * N], U32, name="w_codes%d" % h, align_bytes=64) for h in range(HALVES)]
         w_scales = [held.tile([P, H_EXPERTS * N], U8, name="w_scales%d" % h, align_bytes=64) for h in range(HALVES)]
-
-        def quantize_w(h):
-            nc.vector.quantize_mx(
-                out=w_codes[h][:].bitcast(FP8X4),
-                scales=w_scales[h][:],
-                in_=w_grouped[h][:].rearrange("p e n j -> p (e n j)"),
-            )
 
         def quantize_pair(q):
             h, lo = q // 2, 2 * (q % 2)
@@ -118,12 +96,10 @@ def tile_routed_moe_kernel(tc, xT, w, gate, offs, out):
             nc.vector.quantize_mx(
                 out=x_codes[h][:].bitcast(FP8X4),
                 scales=x_scales[h][:],
-                in_=x_grouped[h][:].rearrange("p n j -> p (n j)"),
+                in_=x_grouped[:, h * H_SLOTS : (h + 1) * H_SLOTS, :].rearrange("p n j -> p (n j)"),
             )
 
-        sums = [held.tile([P, H_SLOTS], F32, name="sums%d" % h) for h in range(HALVES)]
-
-        def multiply(h):
+        def multiply(h, tag):
             acc = psum.tile([P, H_SLOTS], F32, name="acc%d" % h)
             for c in range(H_EXPERTS):
                 cols = slice(c * C, (c + 1) * C)
@@ -136,27 +112,30 @@ def tile_routed_moe_kernel(tc, xT, w, gate, offs, out):
                     start=True,
                     stop=True,
                 )
-            nc.scalar.copy(sums[h][:], acc[:])
+            sums = held.tile([P, H_SLOTS], F32, name=tag, align_bytes=64)
+            nc.scalar.copy(sums[:], acc[:])
+            return sums
 
-        interleave(nc.scalar.copy, 0)
-        interleave(nc.scalar.copy, 1)
-        interleave(nc.scalar.copy, 2)
-        quantize_x(0, "x_codes0")
-        quantize_pair(0)
-        quantize_pair(1)
-        quantize_x(1, "w_raw1")
-        multiply(0)
-        interleave(nc.vector.tensor_copy, 3)
-        quantize_pair(2)
-        quantize_pair(3)
-        multiply(1)
-
-        for h in range(HALVES):
+        def scatter(h, sums):
             nc.vector.tensor_tensor(
                 window[:].indirect(offsets[:, h * H_COLS : (h + 1) * H_COLS]),
-                sums[h][:],
+                sums[:],
                 gate_sb[:, h * H_SLOTS : (h + 1) * H_SLOTS],
                 mult,
             )
+
+        for e in range(7):
+            interleave(nc.scalar.copy, e)
+        quantize_pair(0)
+        quantize_x(0, "w_raw1")
+        quantize_pair(1)
+        quantize_x(1, "w_raw3")
+        sums0 = multiply(0, "w_raw6")
+        interleave(nc.vector.tensor_copy, 7)
+        quantize_pair(2)
+        quantize_pair(3)
+        sums1 = multiply(1, "sums1")
+        scatter(0, sums0)
+        scatter(1, sums1)
 
         nc.sync.dma_start(out, window[:])

@@ -30,14 +30,13 @@ def tile_routed_moe_kernel(tc, xT, w, gate, offs, out):
         held = ctx.enter_context(tc.tile_pool(name="held", bufs=1))
         psum = ctx.enter_context(tc.psum_pool(name="psum", bufs=1))
 
-        offsets = held.tile([P, SLOTS // 16], U16, name="offsets")
+        offsets = held.tile([P, SLOTS // 16], U16, name="offsets", align_bytes=256)
 
         x_view = xT.rearrange("(p t) n -> p t n", t=PACK)
         planes = []
         for t in range(PACK):
-            plane = held.tile([P, T], F32, name="plane%d" % t)
-            nc.sync.dma_start(plane[:, : T // 2], x_view[:, t, : T // 2])
-            nc.sync.dma_start(plane[:, T // 2 :], x_view[:, t, T // 2 :])
+            plane = held.tile([P, T], F32, name="plane%d" % t, align_bytes=256)
+            nc.sync.dma_start(plane[:], x_view[:, t, :])
             planes.append(plane)
             if t == 0:
                 nc.sync.dma_start(offsets[:], offs)
@@ -45,11 +44,11 @@ def tile_routed_moe_kernel(tc, xT, w, gate, offs, out):
         w_view = w.rearrange("e (p j) n -> e p (j n)", j=PACK)
         w_raw = []
         for e in range(E):
-            raw = held.tile([P, PACK, N], F32, name="w_raw%d" % e, align_bytes=64)
+            raw = held.tile([P, PACK, N], F32, name="w_raw%d" % e, align_bytes=256)
             nc.sync.dma_start(raw[:].rearrange("p j n -> p (j n)"), w_view[e])
             w_raw.append(raw)
 
-        gate_sb = held.tile([P, SLOTS], F32, name="gate_sb")
+        gate_sb = held.tile([P, SLOTS], F32, name="gate_sb", align_bytes=256)
         for h in range(HALVES):
             nc.sync.dma_start(gate_sb[:, h * H_SLOTS : (h + 1) * H_SLOTS], gate[:, h * H_SLOTS : (h + 1) * H_SLOTS])
 
@@ -58,7 +57,7 @@ def tile_routed_moe_kernel(tc, xT, w, gate, offs, out):
         nc.gpsimd.memset(warm_in[:], 0.0)
         nc.scalar.copy(warm_out[:], warm_in[:])
 
-        window = held.tile([P, T], F32, name="window")
+        window = held.tile([P, T], F32, name="window", align_bytes=256)
         nc.vector.memset(window[:], 0.0)
 
         x_grouped = held.tile([P, SLOTS, PACK], BF16, name="x_grouped", align_bytes=64)
@@ -91,7 +90,7 @@ def tile_routed_moe_kernel(tc, xT, w, gate, offs, out):
         x_codes, x_scales = [None, None], [None, None]
 
         def quantize_x(h, tag):
-            x_codes[h] = held.tile([P, H_SLOTS], U32, name=tag, align_bytes=64)
+            x_codes[h] = held.tile([P, H_SLOTS], U32, name=tag, align_bytes=256)
             x_scales[h] = held.tile([P, H_SLOTS], U8, name="x_scales%d" % h, align_bytes=64)
             nc.vector.quantize_mx(
                 out=x_codes[h][:].bitcast(FP8X4),
@@ -112,7 +111,7 @@ def tile_routed_moe_kernel(tc, xT, w, gate, offs, out):
                     start=True,
                     stop=True,
                 )
-            sums = held.tile([P, H_SLOTS], F32, name=tag, align_bytes=64)
+            sums = held.tile([P, H_SLOTS], F32, name=tag, align_bytes=256)
             nc.scalar.copy(sums[:], acc[:])
             return sums
 

from contextlib import ExitStack

import concourse.mybir as mybir

K, T, E, C, N = 512, 4096, 8, 128, 128
SLOTS = E * C

FLOPS = 2 * K * N * SLOTS

F32 = mybir.dt.float32
BF16 = mybir.dt.bfloat16
U32 = mybir.dt.uint32
U16 = mybir.dt.uint16
U8 = mybir.dt.uint8
FP8X4 = mybir.dt.float8_e4m3fn_x4

P = 128
PACK = 4
HALVES = 2
H_SLOTS = SLOTS // HALVES
H_EXPERTS = E // HALVES
H_COLS = H_SLOTS // 16


def tile_routed_moe_kernel(tc, xT, w, gate, offs, out):
    nc = tc.nc
    mult = mybir.AluOpType.mult

    with ExitStack() as ctx:
        held = ctx.enter_context(tc.tile_pool(name="held", bufs=1))
        psum = ctx.enter_context(tc.psum_pool(name="psum", bufs=1))

        offsets = held.tile([P, SLOTS // 16], U16, name="offsets", align_bytes=256)

        x_view = xT.rearrange("(p t) n -> p t n", t=PACK)
        planes = []
        for t in range(PACK):
            plane = held.tile([P, T], F32, name="plane%d" % t, align_bytes=256)
            nc.sync.dma_start(plane[:], x_view[:, t, :])
            planes.append(plane)
            if t == 0:
                nc.sync.dma_start(offsets[:], offs)

        w_view = w.rearrange("e (p j) n -> e p (j n)", j=PACK)
        w_raw = []
        for e in range(E):
            raw = held.tile([P, PACK, N], F32, name="w_raw%d" % e, align_bytes=256)
            nc.sync.dma_start(raw[:].rearrange("p j n -> p (j n)"), w_view[e])
            w_raw.append(raw)

        gate_sb = held.tile([P, SLOTS], F32, name="gate_sb", align_bytes=256)
        for h in range(HALVES):
            nc.sync.dma_start(gate_sb[:, h * H_SLOTS : (h + 1) * H_SLOTS], gate[:, h * H_SLOTS : (h + 1) * H_SLOTS])

        warm_in = held.tile([P, 8], F32, name="warm_in")
        warm_out = held.tile([P, 8], F32, name="warm_out")
        nc.gpsimd.memset(warm_in[:], 0.0)
        nc.scalar.copy(warm_out[:], warm_in[:])

        window = held.tile([P, T], F32, name="window", align_bytes=256)
        nc.vector.memset(window[:], 0.0)

        x_grouped = held.tile([P, SLOTS, PACK], BF16, name="x_grouped", align_bytes=64)
        for t in range(PACK):
            nc.vector.tensor_copy(x_grouped[:, :, t], planes[t][:].indirect(offsets[:]))

        w_grouped = [
            held.tile([P, H_EXPERTS, N, PACK], BF16, name="w_grouped%d" % h, align_bytes=64) for h in range(HALVES)
        ]

        def interleave(engine_copy, e):
            dst = w_grouped[e // H_EXPERTS][:, e % H_EXPERTS, :, :]
            src = w_raw[e][:]
            engine_copy(
                dst.rearrange("p (g c i) j -> p g c j i", g=2, i=4),
                src.rearrange("p j (g c i) -> p g c j i", g=2, i=4),
            )

        w_codes = [held.tile([P, H_EXPERTS * N], U32, name="w_codes%d" % h, align_bytes=64) for h in range(HALVES)]
        w_scales = [held.tile([P, H_EXPERTS * N], U8, name="w_scales%d" % h, align_bytes=64) for h in range(HALVES)]

        def quantize_pair(q):
            h, lo = q // 2, 2 * (q % 2)
            nc.vector.quantize_mx(
                out=w_codes[h][:, lo * N : (lo + 2) * N].bitcast(FP8X4),
                scales=w_scales[h][:, lo * N : (lo + 2) * N],
                in_=w_grouped[h][:, lo : lo + 2, :, :].rearrange("p e n j -> p (e n j)"),
            )

        x_codes, x_scales = [None, None], [None, None]

        def quantize_x(h, tag):
            x_codes[h] = held.tile([P, H_SLOTS], U32, name=tag, align_bytes=256)
            x_scales[h] = held.tile([P, H_SLOTS], U8, name="x_scales%d" % h, align_bytes=64)
            nc.vector.quantize_mx(
                out=x_codes[h][:].bitcast(FP8X4),
                scales=x_scales[h][:],
                in_=x_grouped[:, h * H_SLOTS : (h + 1) * H_SLOTS, :].rearrange("p n j -> p (n j)"),
            )

        def multiply(h, tag):
            acc = psum.tile([P, H_SLOTS], F32, name="acc%d" % h)
            for c in range(H_EXPERTS):
                cols = slice(c * C, (c + 1) * C)
                nc.tensor.matmul_mx(
                    out=acc[:, cols],
                    lhsT=w_codes[h][:, cols].bitcast(FP8X4),
                    lhsT_scale=w_scales[h][:, cols],
                    rhs=x_codes[h][:, cols].bitcast(FP8X4),
                    rhs_scale=x_scales[h][:, cols],
                    start=True,
                    stop=True,
                )
            sums = held.tile([P, H_SLOTS], F32, name=tag, align_bytes=256)
            nc.scalar.copy(sums[:], acc[:])
            return sums

        def scatter(h, sums):
            nc.vector.tensor_tensor(
                window[:].indirect(offsets[:, h * H_COLS : (h + 1) * H_COLS]),
                sums[:],
                gate_sb[:, h * H_SLOTS : (h + 1) * H_SLOTS],
                mult,
            )

        for e in range(7):
            interleave(nc.scalar.copy, e)
        quantize_pair(0)
        quantize_x(0, "w_raw1")
        quantize_pair(1)
        quantize_x(1, "w_raw3")
        sums0 = multiply(0, "w_raw6")
        interleave(nc.vector.tensor_copy, 7)
        quantize_pair(2)
        quantize_pair(3)
        sums1 = multiply(1, "sums1")
        scatter(0, sums0)
        scatter(1, sums1)

        nc.sync.dma_start(out, window[:])
